import numpy as np, ml_dtypes
CORES = [16,18,20,22]
N = 4
BF = ml_dtypes.bfloat16
def gentries(a):
    return np.ascontiguousarray(a.reshape(8, 16, -1).transpose(0, 2, 1)).reshape(8, -1)
def gtable(e):
    e = np.asarray(e); return np.ascontiguousarray(e.reshape(8, -1, 16).transpose(0, 2, 1)).reshape(128, -1).astype(np.int32)
R, M, L, F, RO = 512, 512, 3, 512, 3
V = R + L * M
AT = [0] + [R + i * M for i in range(L + 1)]
LEV = np.repeat(np.arange(L + 1), np.diff(AT))
TOP = np.concatenate([2 * np.array(AT)[LEV[R:]], np.full(R, 2 * V)])
LOW = np.array(AT)[LEV + 1]
def under(rng, shape, top):
    return np.minimum((rng.random(shape) * top).astype(np.int64), np.asarray(top) - 1)
def parts(rng):
    i = np.arange(16)[:, None]; sh = (N, 8, 1, V)
    p = rng.integers(0, 16, sh); p2 = (p + rng.integers(1, 16, sh)) % 16
    t = 1 + (255 * rng.random(sh) ** (1.5 + LEV)).astype(np.int64); t2 = 1 + (255 * rng.random(sh) ** (1.5 + LEV)).astype(np.int64)
    x = np.where(i == p, t, 0); x = np.where((i == p2) & (rng.random(sh) < 0.125), t2, x); x = np.where(rng.random(sh) < 0.02, 0, x)
    s = (256 * rng.random((N, 8, 16, R)) ** 1.5).astype(np.int64)
    c = rng.integers(0, 256, (N, 8, 16, R + F)) * (rng.random((N, 8, 16, R + F)) > 0.15)
    half = rng.random(sh) < 0.75
    o = np.argsort(rng.random((N, 8, 16, V)) + 10 * (half & (i >= 8)), axis=2)
    k = np.where(half, rng.choice(np.array([0, 1, 1, 2, 2, 3, 4, 8]), sh), rng.choice(np.array([1, 2, 3, 5, 12, 16]), sh))
    e = np.where(o < k, under(rng, (N, 8, 16, V), TOP), 2 * V)
    a = LOW + under(rng, (N, 8, 2, V), V + R + F - LOW)
    return x, s, c[..., :R].copy(), c[..., R:].copy(), e, a
def rich(rng, x, v):
    k = rng.integers(3, 17, (N, 8, 1, V)); o = np.argsort(rng.random(x.shape), axis=2)
    return np.where(rng.random((N, 8, 1, V)) < 0.25, np.where(o < k, v, 0), x)
def pack(x, s, q, c, e, a):
    def b(v):
        return np.ascontiguousarray(v.reshape(N, 128, -1)).astype(np.float32).astype(BF)
    return {"piv": b(x), "safe": b(s), "lem": b(q), "leaf": b(c), "uses": np.ascontiguousarray(e.reshape(N, 128, V)).astype(np.int32), "prem": np.stack([gtable(v) for v in a.reshape(N, 8, 2 * V)])}
def setup_inputs(rng):
    return pack(*parts(rng))
def setup_inputs_turn(rng):
    x, s, q, c, e, a = parts(rng); i = np.arange(16)[:, None]
    j = rng.integers(0, 16, (N, 8, 1, 1)); w = rng.integers(0, 7, (N, 8, 1, V))
    w[..., :7] = np.arange(7)
    one, two = i == j, i == (j + 8) % 16
    m = np.where(w == 0, one, np.where(w == 1, two, np.where(w == 2, one | two, np.where(w == 3, i < 8, np.where(w == 4, i >= 8, w == 5)))))
    n = under(rng, (N, 8, 16, V), TOP); n = n - (n & 1) * (rng.random(n.shape) < 0.5)
    x = np.where(rng.random((N, 8, 1, V)) < 0.3, 0, x)
    return pack(x, s, q, c, np.where(m, n, 2 * V), a)
def setup_inputs_ties(rng):
    x, s, q, c, e, a = parts(rng); v = np.array([0, 1, 127, 128, 129, 254, 255])
    x = rich(rng, x, 1)
    x = np.where(x > 0, rng.choice(np.array([1, 127, 128, 129, 255]), x.shape), 0); nx = np.roll(x, 8, axis=2)
    s, q, c = rng.choice(v, s.shape), rng.choice(v, q.shape), rng.choice(v, c.shape)
    s[..., 0] = x[..., 0]; s[..., 1] = np.maximum(x[..., 1] - 1, 0); s[..., 2] = np.maximum(x[..., 2], nx[..., 2]); s[..., 3] = nx[..., 3]
    return pack(x, s, q, c, e, a)
def setup_inputs_alike(rng):
    x, s, q, c, e, a = parts(rng); on = e < 2 * V
    e[:, 1] = np.where(on[:, 1], under(rng, (N, 1, V), TOP), 2 * V)
    e[:, 2] = np.where(on[:, 2], np.where(rng.random((N, 16, V)) < 0.5, 0, TOP - 1), 2 * V)
    e[:, 3] = 2 * V
    e[:, 4] = np.where(on[:, 4], TOP - 1 - rng.integers(0, 16, (N, 16, V)), 2 * V)
    e[:, 5] = under(rng, (N, 16, V), TOP)
    a[:, 1, 1] = a[:, 1, 0]; a[:, 2] = np.where(rng.random((N, 2, V)) < 0.5, LOW, V + R + F - 1)
    a[:, 4] = V + rng.integers(0, R, (N, 2, V)); a[:, 5] = V + R + rng.integers(0, F, (N, 2, V)); a[:, 6] = LOW
    return pack(x, s, q, c, e, a)
def setup_inputs_late(rng):
    x, s, q, c, e, a = parts(rng); g = int(rng.integers(0, 8)); s[:] = 0
    q2, c2 = rng.integers(200, 256, q.shape), rng.integers(200, 256, c.shape); q2[:, g] = q[:, g]; c2[:, g] = c[:, g]
    e[..., V - R:] = np.where(rng.random((N, 8, 1, R)) < 0.5, 2 * V, e[..., V - R:])
    return pack(x, s, q2, c2, e, a)
def setup_inputs_spread(rng):
    x, s, q, c, e, a = parts(rng)
    def u(n):
        return np.minimum((np.exp2(8 * rng.random((N, 8, 1, n))) * rng.random((N, 8, 16, n))).astype(np.int64), 255)
    x = np.where(x > 0, np.minimum(np.exp2(8 * rng.random(x.shape)).astype(np.int64), 255), 0)
    x = rich(rng, x, np.maximum(u(V), 1))
    m = rng.random((N, 8, 16, V)) < rng.random((N, 8, 1, V)) ** 3
    return pack(x, u(R), u(R), u(F), np.where(m, under(rng, (N, 8, 16, V), TOP), 2 * V), a)
def check_inputs(d):
    bad = []
    for k in ("piv", "safe", "lem", "leaf"):
        v = np.asarray(d[k]).astype(np.float32)
        if not np.all((v >= 0) & (v <= 255) & (v == np.floor(v))): bad.append("whole numbers from 0 to 255 in " + k)
    e = np.asarray(d["uses"]).astype(np.int64)
    if not np.all(((e >= 0) & (e < TOP)) | (e == 2 * V)): bad.append("range of uses")
    a = np.stack([gentries(v) for v in d["prem"]]).astype(np.int64).reshape(N, 8, 2, V)
    if not np.all((a >= LOW) & (a < V + R + F)): bad.append("range of prem")
    return bad
def least(S, e):
    return np.stack([[np.min(np.take(S[q, g], e[q, g], axis=1), axis=1) for g in range(8)] for q in range(N)])
def splice(e, st):
    K = np.zeros((N, 8, 1, 2 * V + 1), bool)
    K[:, :, 0, 2 * R:2 * V:2] = st[..., R:] == 1; K[:, :, 0, 2 * R + 1:2 * V:2] = st[..., R:] == 2
    loose = np.take_along_axis(K, e, 3); has = np.any(loose, axis=2, keepdims=True); j = np.argmax(loose, axis=2)[:, :, None]
    this = (np.arange(16)[:, None] == j) & has
    u = np.take_along_axis(e, j, 2) >> 1
    t = np.roll(np.take_along_axis(e, np.where(has, u - R, 0), 3), 8, axis=2)
    hit = np.any((t != 2 * V) & (e != 2 * V) & ~this, axis=2, keepdims=True)
    return np.where(has & ~hit, np.where(t != 2 * V, t, np.where(this, 2 * V, e)), e)
def reference(piv, safe, lem, leaf, uses, prem):
    def w(v):
        return v.astype(np.float32).astype(np.int64).reshape(N, 8, 16, -1)
    x = w(piv); nx = np.roll(x, 8, axis=2)
    s = np.full((N, 8, 16, V), 255, np.int64); s[..., :R] = w(safe)
    C = np.zeros((N, 8, 16, V + R + F), np.int64); C[..., V:V + R] = w(lem); C[..., V + R:] = w(leaf)
    e = uses.astype(np.int64).reshape(N, 8, 16, V)
    a = np.stack([gentries(v) for v in prem]).astype(np.int64).reshape(N, 8, 2, V)
    st = np.zeros((N, 8, V), np.int64); S = np.full((N, 8, 16, 2 * V + 1), 255, np.int64); gs = None
    for rnd in range(RO):
        old = st[:, :, None] > 0
        if rnd:
            s[..., :R] = np.where(old[..., :R], s[..., :R], np.roll(gs, 1, axis=0))
            C[..., V:V + R] = np.roll(C[..., :R], -1, axis=0)
            e = splice(e, st)
        for l in range(L + 1):
            i, j = AT[l], AT[l + 1]
            if l: s[..., i:j] = np.where(old[..., i:j], s[..., i:j], least(S, e[..., i - R:j - R]))
            y, p, n = s[..., i:j], x[..., i:j], nx[..., i:j]; b = st[..., i:j]
            b = np.where(b > 0, b, np.where(np.all(y >= p, axis=2), 1, np.where(np.all(y >= n, axis=2), 2, 0)))
            st[..., i:j] = b; b = b[:, :, None]
            S[..., 2 * i:2 * j:2] = np.where(b == 0, np.maximum(y, p), np.where(b == 1, y, 255))
            S[..., 2 * i + 1:2 * j:2] = np.where(b == 0, np.maximum(y, n), np.where(b == 2, y, 255))
        gs = least(S, e[..., V - R:])
        for l in range(L, -1, -1):
            i, j = AT[l], AT[l + 1]; p, n = x[..., i:j], nx[..., i:j]; b = st[..., i:j]
            A = np.take_along_axis(C, a[:, :, :1, i:j], 3); B = np.take_along_axis(C, a[:, :, 1:, i:j], 3)
            b = np.where(b > 0, b, np.where(~np.all(A >= p, axis=2), 1, np.where(~np.all(B >= n, axis=2), 2, 0)))
            st[..., i:j] = b; b = b[:, :, None]
            C[..., i:j] = np.where(b == 1, A, np.where(b == 2, B, np.maximum(np.where(p > 0, 0, A), np.where(n > 0, 0, B))))
    return {"yc": np.ascontiguousarray(C[..., :V]).reshape(N, 128, V).astype(np.float32).astype(BF), "ys": np.concatenate([s, gs], axis=3).reshape(N, 128, V + R).astype(np.float32).astype(BF)}

from concourse.mybir import AluOpType as A, ActivationFunctionType as AF

PW = 128
CWM = 256
CH = {l: [(512 * l, 256), (512 * l + 256, 256)] for l in range(4)}
SW = 512
NG, NSO, NFG, NMP = 6, 3, 4, 4
MAINB, SPLB = 5, 3
NB16 = 28
SCRATCH = {
    "raw": ("sbuf", [128, 2048], "int32"), "rpm": ("sbuf", [128, 256], "int32"), "po": ("sbuf", [128, 256], "uint16"),
    "off": ("sbuf", [128, 2048], "uint16"), "lt0": ("sbuf", [128, 2056], "float32"), "lt1": ("sbuf", [128, 2056], "float32"),
    "F": ("sbuf", [128, 4112], "bfloat16"), "Z": ("sbuf", [128, 4112], "bfloat16"),
    "xm": ("sbuf", [128, 4096], "bfloat16"), "zx": ("sbuf", [128, 4096], "bfloat16"),
    "o": ("sbuf", [128, 2560], "bfloat16"), "ko": ("sbuf", [128, 2048], "bfloat16"), "st": ("sbuf", [128, 2048], "bfloat16"),
    "sf": ("sbuf", [128, 512], "bfloat16"), "as1": ("sbuf", [128, 512], "bfloat16"), "as2": ("sbuf", [128, 512], "bfloat16"),
    "ob": ("sbuf", [128, 128], "bfloat16"), "of": ("sbuf", [128, 128], "float32"), "tb": ("sbuf", [128, 128], "bfloat16"), "tf": ("sbuf", [128, 128], "float32"),
    "ones": ("sbuf", [128, 512], "bfloat16"), "mb": ("sbuf", [128, 128 * NB16], "bfloat16"), "mf": ("sbuf", [128, 128 * 17], "float32"), "blf": ("sbuf", [128, 128], "float32"),
    "m1": ("sbuf", [128, 2048], "bfloat16"), "ip": ("sbuf", [128, 16], "int32"), "pw": ("sbuf", [128, 16], "float32"),
    "yo": ("sbuf", [128, 2560], "bfloat16"),
}
for _k in range(3): SCRATCH["cw%d" % _k] = ("sbuf", [128, 3072], "bfloat16")
for _k in range(NG): SCRATCH["g%d" % _k] = ("sbuf", [128, PW * 16], "bfloat16")
for _k in range(NFG): SCRATCH["fg%d" % _k] = ("sbuf", [128, PW * 16], "bfloat16")
for _k in range(NSO): SCRATCH["so%d" % _k] = ("sbuf", [128, CWM * 16], "bfloat16")
for _k in range(NMP): SCRATCH["mp%d" % _k] = ("sbuf", [128, PW * 16], "bfloat16")
for _k in range(3):
    for _n, _w in (("ab", 2 * CWM), ("tt", 2 * CWM), ("vv", CWM), ("mm", CWM), ("bb", CWM), ("ww", CWM)): SCRATCH["%s%d" % (_n, _k)] = ("sbuf", [128, _w], "bfloat16")
for _k in range(2):
    for _n in ("X", "L1", "Tg", "dl"): SCRATCH["%s%d" % (_n, _k)] = ("sbuf", [128, SW], "float32")
    for _n in ("ge", "hm"): SCRATCH["%s%d" % (_n, _k)] = ("sbuf", [128, SW], "bfloat16")
    SCRATCH["xi%d" % _k] = ("sbuf", [128, SW // 16], "int32")
    SCRATCH["xu%d" % _k] = ("sbuf", [128, SW // 16], "uint16")
for _k in range(8): SCRATCH["ps%d" % _k] = ("psum", [128, 512], "float32")
NDMA = 60
QS = ("vector", "scalar", "tensor", "pool")
SEMAPHORES = ["q_" + q for q in QS] + ["d%d" % k for k in range(NDMA)] + ["ra%d" % k for k in range(4)] + ["la%d" % k for k in range(4)]

CY = 0.00083
OV = {"vector": 0.06, "scalar": 0.07, "tensor": 0.02, "pool": 0.15, "sync": 0.1}
PEC = 0.00055
WAKE = 0.12
SZ = {"float32": 4, "int32": 4, "bfloat16": 2, "uint16": 2}
GC = 1.5
ASG = "1000110001010100000111001100000110100011100000010010111000000001001010010000101001100010110000000000101110100101101010000000000000101001001000011011100100100000110000001001010010000011001100000000100000001000000101001001001"
OFFS = {'1 down2g': -3, '0 up1k': -2, '1 down0t': 19, '1 up0k': 17, '1 up0t': 10, '1 up0v': 20, '0 up0g': 14, '0 ghostsg': -15, '0 ghostsv': -28,
        '1 splice4g': 4, '2 up2g': 15, '2 up2y': -12, '1 down3t': -10, '1 down3v': -12, '2 ghostsg': -12, '2 splice3t': -4, '2 splice4g': -45,
        '2 down0v': 9, 'initv': -3, '0 down3v': -16, '1 up1t': -2, '1 up1v': 1, '1 splice2v': 8, '2 up1y': 19, '2 down1t': 2, '0 up2t': 5,
        '1 down1t': -6, '1 down0v': -1, '1 splice2g': -9, '1 splice3v': -2, '2 up1t': 2, '0 up0v': 1, '1 splice3g': -6, '1 splice3t': -12}
PLAN = {}


def conflict(a, b):
    if a[1] >= b[2] or b[1] >= a[2]: return False
    return not (a[3] == 2 and b[3] == 2 and (a[1] - b[1]) % 2)


def build(T, rank, topo, core):
    ops = []
    last = {}
    ndma = [0]
    ph = ["init"]

    def ap(r):
        t = T[r[0]]
        return t[:, r[1]:r[2]] if r[3] == 1 else t[:, r[1]:r[2]:r[3]]

    def R(name, lo=0, hi=None, st=1):
        return (name, lo, SCRATCH[name][1][1] if hi is None else hi, st)

    def n_of(r): return (r[2] - r[1] + r[3] - 1) // r[3]

    def isps(r): return SCRATCH[r[0]][0] == "psum"

    def sz(r): return SZ[SCRATCH[r[0]][2]]

    def op(opts, rd, wr, sem=None, kind="v"):
        i = len(ops)
        deps = {}
        qs = set(o[0] for o in opts)
        for w, lst in ((0, rd), (1, wr)):
            for r in lst:
                for (j, rr, ww) in last.setdefault(r[0], []):
                    if j == i: continue
                    if isps(r):
                        if qs == {"tensor"} and ops[j]["qs"] == {"tensor"}: k = "acc"
                        else: k = "w" if (w or ww) and conflict(r, rr) else "ord"
                    else:
                        if not (w or ww) or not conflict(r, rr): continue
                        k = "w"
                    if deps.get(j) != "w": deps[j] = k
        ops.append(dict(opts=opts, deps=deps, sem=sem, qs=qs, name=ph[0] + kind))
        for w, lst in ((1, wr), (0, rd)):
            for r in lst:
                h = last[r[0]]
                if w and not isps(r) and r[3] == 1: h[:] = [e for e in h if not (r[1] <= e[1][1] and e[1][2] <= r[2])]
                h.append((i, r, w))
        return i

    cut = {}
    rot = {}

    def bank(pool):
        n, base = (MAINB, 0) if pool == "m" else (SPLB, MAINB)
        k = rot.get(pool, 0); rot[pool] = k + 1
        b = "ps%d" % (base + k % n)
        h = last.setdefault(b, [])
        h[:] = h[cut.get(b, 0):]
        cut[b] = len(h)
        return b

    def pick(name, n):
        k = rot.get(name, 0); rot[name] = k + 1
        return "%s%d" % (name, k % n)

    def cv(n, per): return max(64, n * per) * CY + OV["vector"]

    def tt(out, a, b, f, **k):
        per = 1 if (isps(a) or isps(b)) else 2
        return op([("vector", cv(n_of(out), per), lambda e: e.tensor_tensor(ap(out), ap(a), ap(b), f))], [a, b], [out], **k)

    def vts(out, a, s1, s2, f, f2=None):
        per = 0.5 if (sz(out) == 2 and sz(a) == 2) else 1
        kw = {} if f2 is None else {"op1": f2}
        return ("vector", cv(n_of(out), per), lambda e: e.tensor_scalar(ap(out), ap(a), ap(s1) if isinstance(s1, tuple) else s1, s2, op0=f, **kw))

    def act(out, a, f, bias=0.0, scale=1.0):
        return ("scalar", max(64, n_of(out)) * CY + OV["scalar"], lambda e: e.activation(ap(out), ap(a), f, bias=bias, scale=scale))

    def ts(out, a, s1, s2, f, f2=None, **k):
        return op([vts(out, a, s1, s2, f, f2)], [a] + ([s1] if isinstance(s1, tuple) else []), [out], **k)

    def flex(out, a, o1, o2, **k): return op([o1, o2], [a], [out], **k)

    def vcopy(out, a):
        per = 0.5 if (sz(out) == 2 and sz(a) == 2) else 1
        return ("vector", cv(n_of(out), per), lambda e: e.tensor_copy(ap(out), ap(a)))

    def copy(out, a, **k): return op([vcopy(out, a)], [a], [out], **k)

    def fcopy(out, a, **k): return flex(out, a, act(out, a, AF.Copy), vcopy(out, a), **k)

    def mset(out, c, **k):
        return op([("vector", cv(n_of(out), 0.5), lambda e: e.memset(ap(out), c))], [], [out], **k)

    def mm(lst, **k):
        def fn(e):
            for (o_, l_, r_, s_, t_) in lst: ins = e.matmul(ap(o_), ap(l_), ap(r_), s_, t_)
            return ins
        us = sum(max(64, n_of(o_)) * (4 if sz(l_) == 4 else 1) * PEC + OV["tensor"] for (o_, l_, r_, s_, t_) in lst)
        rd, wr = [], []
        for (o_, l_, r_, s_, t_) in lst:
            for z, y in ((l_, rd), (r_, rd), (o_, wr)):
                if z not in y: y.append(z)
        return op([("tensor", us, fn)], rd, wr, kind="t", **k)

    def gather(out, win, offs_, relu):
        n = n_of(out)
        if relu:
            fv = lambda e: e.tensor_scalar(ap(out), ap(win).indirect(ap(offs_)), -1.0, 0.0, op0=A.mult, op1=A.max)
            fs = lambda e: e.activation(ap(out), ap(win).indirect(ap(offs_)), AF.Relu, scale=-1.0)
        else:
            fv = lambda e: e.tensor_copy(ap(out), ap(win).indirect(ap(offs_)))
            fs = lambda e: e.activation(ap(out), ap(win).indirect(ap(offs_)), AF.Copy)
        return op([("scalar", n * GC * CY + OV["scalar"], fs), ("vector", n * GC * CY + OV["vector"], fv)], [win, offs_], [out], kind="g")

    def scan(out, g_, m_):
        return op([("vector", cv(n_of(out), 0.5), lambda e: e.tensor_tensor_scan(ap(out), ap(g_), ap(m_), 0.0, A.max, A.mult))], [g_, m_], [out])

    def dma(q, out, in_, rd, wr):
        s = "d%d" % ndma[0]; ndma[0] += 1
        return op([(q, OV["sync"], lambda e: e.dma_start(out(), in_()))], rd, wr, sem=(s, 16))

    def load(q, r, src, lo, hi): return dma(q, lambda: ap(r), lambda: T[src][:, lo:hi], [], [r])

    def store(q, dst, lo, hi, r): return dma(q, lambda: T[dst][:, lo:hi], lambda: ap(r), [r], [])

    def local(q, r, s): return dma(q, lambda: ap(r), lambda: ap(s), [s], [r])

    MB = {}

    def mat(nm): return R("mb", MB[nm] * 128, MB[nm] * 128 + 128)

    def newmat(nm):
        MB[nm] = len(MB)
        return mat(nm)

    def matf(k): return R("mf", k * 128, k * 128 + 128)

    load("sync", R("raw", 0, 512), "uses", 0, 512)
    load("scalar", R("yo", 0, 512), "piv", 0, 512)
    load("sync", R("sf"), "safe", 0, 512)
    load("scalar", R("rpm"), "prem", 0, 256)
    for l in range(1, 4):
        load("sync", R("yo", 512 * l, 512 * l + 512), "piv", 512 * l, 512 * l + 512)
        load("sync", R("raw", 512 * l, 512 * l + 512), "uses", 512 * l, 512 * l + 512)
    load("sync", R("cw0", 2560, 3072), "leaf", 0, 512)
    load("sync", R("cw0", 2048, 2560), "lem", 0, 512)

    def gsel(out, src, pattern, cmp, base, cm):
        def fn(e): return e.affine_select(ap(out), ap(src), pattern, cmp, 0.0, base, cm)
        return op([("pool", 0.17 + 256 * CY + 0.05, fn)], [src], [out])
    mset(R("ob"), 1.0)
    gsel(newmat("P"), R("ob"), [[-16, 8], [8, 2], [-1, 8]], A.is_equal, -8, 1)
    gsel(newmat("I"), R("ob"), [[-1, 128]], A.is_equal, 0, 1)
    gsel(R("tb"), R("ob"), [[-16, 8], [0, 16]], A.is_ge, 0, 1)
    gsel(newmat("B"), R("tb"), [[16, 8], [0, 16]], A.is_ge, 15, -1)
    gsel(newmat("sub"), mat("B"), [[-1, 128]], A.is_equal, 1, 1)

    def scaled(nm, src, c):
        o_ = newmat(nm)
        return flex(o_, mat(src), act(o_, mat(src), AF.Copy, scale=float(c)), vts(o_, mat(src), float(c), None, A.mult))
    mset(R("ones"), 1.0)
    for nm, s_, c in (("B2", "B", 2), ("Bn16", "B", -0.0625), ("I5", "I", 512), ("In5", "I", -512), ("Bn2", "B", -2), ("B16", "B", 0.0625)): scaled(nm, s_, c)
    mset(R("m1"), 1.0); mset(R("m1", 15, 2048, 16), -1.0)
    mset(R("F"), 0.0)

    def pair(l):
        for n0, w in CH[l]:
            a, b = R("xm", 2 * n0, 2 * n0 + w), R("xm", 2 * n0 + w, 2 * n0 + 2 * w)
            ts(a, R("yo", n0, n0 + w), -255.0, None, A.add)
            p = R(bank("m"), 0, w)
            mm([(p, mat("P"), a, True, True)])
            fcopy(b, p)

    def zero(l): ts(R("zx", 1024 * l, 1024 * l + 1024), R("xm", 1024 * l, 1024 * l + 1024), -255.0, -255.0, A.is_gt, A.mult)

    def offs(l): copy(R("off", 512 * l - 512, 512 * l), R("raw", 512 * l - 512, 512 * l))

    def late_consts():
        ts(R("cw0", 2048, 3072), R("cw0", 2048, 3072), -255.0, None, A.add)
        for k in (1, 2): local("sync", R("cw%d" % k, 2560, 3072), R("cw0", 2560, 3072))
        for k in range(NMP): local("sync", R("mp%d" % k), R("m1"))
        mset(R("Z"), 0.0)
        mset(R("of"), 1.0)
        gsel(R("tf"), R("of"), [[-16, 8], [0, 16]], A.is_ge, 0, 1)
        gsel(R("blf"), R("tf"), [[16, 8], [0, 16]], A.is_ge, 15, -1)
        gsel(matf(16), R("of"), [[-16, 8], [8, 2], [-1, 8]], A.is_equal, -8, 1)
        for q in range(16): gsel(matf(q), R("blf"), [[0, 8], [1, 16]], A.is_equal, -q, 0)
        for i in range(16): scaled("D%d" % i, "I", 2.0 ** (15 - i))
        tt(newmat("S1"), mat("I"), mat("sub"), A.subtract)
        tt(newmat("Sn"), mat("sub"), mat("I"), A.subtract)
        op([("pool", 0.2, lambda e: e.iota(T["ip"][:, 0:1], [[0, 1]], 0, 1))], [], [R("ip", 0, 1)])
        for k, f in ((0, 2), (1, 4), (2, 16), (3, 256)):
            ts(R("ip", 1 + k, 2 + k), R("ip", 0, 1), 1 << k, None, A.bitwise_and)
            ts(R("pw", 1 + k, 2 + k), R("ip", 1 + k, 2 + k), -(f - 1) / float(1 << k), float(f), A.mult, A.add)
        tt(R("pw", 5, 6), R("pw", 1, 2), R("pw", 2, 3), A.mult)
        tt(R("pw", 6, 7), R("pw", 3, 4), R("pw", 4, 5), A.mult)
        tt(R("pw", 0, 1), R("pw", 5, 6), R("pw", 6, 7), A.mult)
        for l in range(1, 5):
            a = 512 * (l - 1) + (8 if l == 4 else 0)
            ts(R("lt0", a, a + 512), R("raw", 512 * l - 512, 512 * l), -1.0, 4096.0, A.mult, A.add)
            if l == 1: ts(R("lt1", a, a + 512), R("raw", 0, 512), -1.0, 4096.0, A.mult, A.add)
        for z in ("lt0", "lt1"): mset(R(z, 1536, 1544), 0.0)

    def thr(tab, n0, w, sign, both=True):
        b = bank("m")
        mm([(R(b, 0, 2 * w), mat("I"), R(tab, 2 * n0, 2 * n0 + 2 * w), True, not both)])
        if both:
            s_ = R("st", n0, n0 + w)
            p, m = (mat("I5"), mat("In5")) if sign > 0 else (mat("In5"), mat("I5"))
            return b, lambda: mm([(R(b, 0, w), p, s_, False, False), (R(b, w, 2 * w), m, s_, False, True)])
        return b, None

    def counts(w, first, second, t):
        b = bank("m")
        mm([(R(b, 0, w), mat(first), R("ones", 0, w), True, False)])
        mm([(R(b, 0, w), mat(second), R(t, 0, w), False, True), (R(b, w, 2 * w), mat("B"), R(t, w, 2 * w), True, True)])
        return b

    def tests(rnd, n0, w, osrc):
        n1 = n0 + w
        nb, fin = thr("xm", n0, w, 1, rnd > 0)
        if fin: fin()
        t = pick("tt", 3)
        tt(R(t, 0, w), osrc, R(nb, 0, w), A.is_lt)
        tt(R(t, w, 2 * w), osrc, R(nb, w, 2 * w), A.is_lt)
        cb = counts(w, "Bn16", "B2", t)
        v = R(pick("vv", 3), 0, w)
        c = R(cb, w, 2 * w)
        flex(v, c, act(v, c, AF.Relu, bias=1.0, scale=-1.0), vts(v, c, 0.0, None, A.is_equal))
        n2, fin = thr("xm", n0, w, 1)
        tt(R("st", n0, n1), v, R(cb, 0, w), A.min)
        fin()
        return n2

    def edges(n0, w, n2):
        n1 = n0 + w
        tt(R("F", 2 * n0, 2 * n1, 2), R("o", n0, n1), R(n2, 0, w), A.max)
        tt(R("F", 2 * n0 + 1, 2 * n1, 2), R("o", n0, n1), R(n2, w, 2 * w), A.max)

    def plus(a, b): flex(a, b, act(a, b, AF.Copy, bias=255.0), vts(a, b, 255.0, None, A.add), kind="y")

    def out_s(lo, hi):
        plus(R("yo", lo, hi), R("o", lo, hi)); store("sync", "ys", lo, hi, R("yo", lo, hi))

    def down0(rnd):
        ph[0] = "%d down0" % rnd
        for n0, w in CH[0]:
            n1 = n0 + w
            if rnd == 0: ts(R("o", n0, n1), R("sf", n0, n1), -255.0, None, A.add)
            else:
                w_, z = R(pick("ww", 3), 0, w), R(pick("bb", 3), 0, w)
                ts(w_, R("st", n0, n1), 0.0, None, A.is_equal)
                tt(z, R("as%d" % rnd, n0, n1), w_, A.mult)
                tt(R("o", n0, n1), z, R("ko", n0, n1), A.add)
            edges(n0, w, tests(rnd, n0, w, R("o", n0, n1)))
        if rnd == 2: out_s(0, 512)

    def pieces(rnd, col, n0, w, so):
        for p in range(0, w, PW):
            gb = R(pick("g", NG))
            gather(gb, R("F", 0, 4097), R("off", col + p, col + p + PW), True)
            if n0 is None or rnd == 0: m_ = R("m1")
            else:
                mp = pick("mp", NMP)
                ts(R(mp, 15, PW * 16, 16), R("st", n0 + p, n0 + p + PW), 0.0, -1.0, A.is_equal, A.mult)
                m_ = R(mp)
            scan(R(so, p * 16, (p + PW) * 16), gb, m_)

    def down(rnd, l):
        ph[0] = "%d down%d" % (rnd, l)
        todo = []
        for n0, w in CH[l]:
            n1 = n0 + w
            so = pick("so", NSO)
            pieces(rnd, n0 - 512, n0, w, so)
            last_ = R(so, 15, w * 16, 16)
            o_ = R("o", n0, n1)
            todo.append((n0, w, tests(rnd, n0, w, last_)))
            if rnd == 0: fcopy(o_, last_)
            else: tt(o_, last_, R("ko", n0, n1), A.add)
        for z in todo: edges(*z)
        if rnd == 2: out_s(512 * l, 512 * l + 512)

    nremote = [0]

    def send(src, dst, to):
        k = nremote[0]; nremote[0] += 1
        d = T.cores[to % 4]
        rid, pid = topo.addr(d)[:2]
        mask = sum(1 << e for e in topo.engines(core, d)[:8])
        i = op([("pool", 1.0, lambda e: e.remote_dma(ap(dst), ap(src), T.sem["ra%d" % k], T.sem["la%d" % k], pid, rid, mask))], [src], [], sem=("la%d" % k, 8))
        j = op([(None, 5.0, None)], [], [dst], sem=("ra%d" % k, 8))
        ops[j]["after"] = i

    def ghosts(rnd):
        ph[0] = "%d ghosts" % rnd
        for c in range(0, 512, CWM):
            so = pick("so", NSO)
            pieces(rnd, 1536 + c, None, CWM, so)
            fcopy(R("o", 2048 + c, 2048 + c + CWM), R(so, 15, CWM * 16, 16))
        if rnd < 2: send(R("o", 2048, 2560), R("as%d" % (rnd + 1)), rank + 1)
        else: out_s(2048, 2560)

    def up(rnd, l):
        ph[0] = "%d up%d" % (rnd, l)
        cw = "cw%d" % rnd
        for n0, w in CH[l]:
            n1, c = n0 + w, n0 // 8
            ab = pick("ab", 3); a_, b_ = R(ab, 0, w), R(ab, w, 2 * w)
            gather(R(ab, 0, 2 * w), R(cw, 512 * l + 512, 3072), R("po", c, c + w // 8), False)
            xb, fin = thr("xm", n0, w, -1)
            fin()
            t = pick("tt", 3)
            tt(R(t, 0, 2 * w), R(ab, 0, 2 * w), R(xb, 0, 2 * w), A.is_lt)
            fb = counts(w, "B16", "Bn2", t)
            v = R(pick("vv", 3), 0, w); f_ = R(fb, w, 2 * w)
            flex(v, f_, act(v, f_, AF.Sign), vts(v, f_, 1.0, None, A.min))
            tb, fin = thr("zx", n0, w, -1)
            tt(R("st", n0, n1), v, R(fb, 0, w), A.min)
            fin()
            m_ = R(pick("mm", 3), 0, w)
            tt(R(tb, 0, w), a_, R(tb, 0, w), A.min)
            tt(m_, b_, R(tb, w, 2 * w), A.min)
            tt(R(cw, n0, n1), m_, R(tb, 0, w), A.max)
            if rnd < 2:
                if l:
                    ts(R("Z", 2 * n0, 2 * n1, 2), R("st", n0, n1), 0.0, None, A.is_lt, kind="z")
                    zb = R("Z", 2 * n0 + 1, 2 * n1, 2)
                    flex(zb, R("st", n0, n1), act(zb, R("st", n0, n1), AF.Relu), vts(zb, R("st", n0, n1), 0.0, None, A.is_gt), kind="z")
                z = R(pick("bb", 3), 0, w)
                ts(z, R("st", n0, n1), 0.0, None, A.not_equal, kind="k")
                tt(R("ko", n0, n1), R("o", n0, n1), z, A.mult, kind="k")
            else:
                plus(R("ko", n0, n1), R(cw, n0, n1)); store("sync", "yc", n0, n1, R("ko", n0, n1))
        if rnd < 2 and l == 0: send(R(cw, 0, 512), R("cw%d" % (rnd + 1), 2048, 2560), rank - 1)

    def splice(k, l):
        ph[0] = "%d splice%d" % (k + 1, l)
        src, dst = ("lt0", "lt1") if k == 0 else ("lt1", "lt0")
        for c in range(0, 512, SW):
            w = SW
            col = 512 * (l - 1) + c
            lc = col + (8 if l == 4 else 0)
            L = R(src, lc, lc + w)
            mk = bank("s")
            for p in range(0, w, PW):
                fg = pick("fg", NFG)
                gather(R(fg), R("Z", 0, 4097), R("off", col + p, col + p + PW), False)
                for h in range(0, 16, 4): mm([(R(mk, p, p + PW), mat("D%d" % i), R(fg, i, PW * 16, 16), i == 0, i == 15) for i in range(h, h + 4)])
            ge = R(pick("ge", 2))
            ts(ge, R(mk, 0, w), R("pw", 0, 1), None, A.is_ge)
            th = R(bank("s"), 0, w)
            mm([(th, mat("S1"), ge, True, True)])
            X = pick("X", 2)
            tt(R(X), L, th, A.mult)
            wr = R(bank("s"), 0, w // 16)
            for h in range(0, 16, 4): mm([(wr, matf(q), R(X, q, w, 16), q == 0, q == 15) for q in range(h, h + 4)])
            xi, xu = R(pick("xi", 2)), R(pick("xu", 2))
            ts(xi, wr, -0.5, 1535.75, A.mult, A.add)
            copy(xu, xi)
            nt = R(bank("s"), 0, w)
            mm([(nt, mat("B16"), R("ones", 0, w), True, False), (nt, mat("Sn"), ge, False, True)])
            L1 = R(pick("L1", 2))
            tt(L1, L, nt, A.mult)
            tg = pick("Tg", 2)
            gather(R(tg), R(src, 0, 1544), xu, False)
            tp = bank("s")
            for h in range(0, w, 128): mm([(R(tp, h, h + 128), matf(16), R(tg, h, h + 128), True, True)])
            h = R(pick("hm", 2))
            tp = R(tp, 0, w)
            tt(h, L1, tp, A.min)
            ht = R(bank("s"), 0, w)
            mm([(ht, mat("B"), h, True, True)])
            dl = R(pick("dl", 2))
            tt(dl, tp, R(X), A.subtract)
            flex(ht, ht, act(ht, ht, AF.Relu, bias=1.0, scale=-1.0), vts(ht, ht, 0.0, None, A.is_equal))
            tt(ht, dl, ht, A.mult)
            tt(R(dst, lc, lc + w), L, ht, A.add)
            ts(R("off", col, col + w), R(dst, lc, lc + w), -1.0, 4096.0, A.mult, A.add)

    pair(0)
    down0(0)
    for l in (1, 2, 3):
        ph[0] = "init"
        offs(l); pair(l)
        down(0, l)
    ph[0] = "init"
    offs(4)
    for l in (3, 2, 1, 0): zero(l)
    for l in range(4):
        for n0, w in CH[l]:
            for z in range(2): ts(R("po", n0 // 8 + z * w // 16, n0 // 8 + (z + 1) * w // 16), R("rpm", 128 * z + n0 // 16, 128 * z + (n0 + w) // 16), -512.0 * (l + 1), None, A.add)
    ph[0] = "late"
    late_consts()
    for rnd in range(3):
        if rnd:
            for l in (2, 3, 4): splice(rnd - 1, l)
            down0(rnd)
            for l in (1, 2, 3): down(rnd, l)
        ghosts(rnd)
        for l in (3, 2, 1, 0): up(rnd, l)
    return ops


def flexes(ops): return [i for i, o in enumerate(ops) if len(o["opts"]) == 2]


def assign_of(ops, s):
    fl = flexes(ops)
    a = [o["opts"][0][0] for o in ops]
    for k, i in enumerate(fl): a[i] = "vector" if (s[k] == "1" if s else k % 3 == 0) else "scalar"
    return a


def plan(ops, asg, offs):
    n = len(ops)
    us = [[x[1] for x in o["opts"] if x[0] == asg[i]][0] for i, o in enumerate(ops)]
    lat = [2.5 if o["sem"] else 0.0 for o in ops]
    succ = [[] for _ in range(n)]
    left = [0] * n
    for i, o in enumerate(ops):
        p = set(o["deps"])
        if "after" in o: p.add(o["after"])
        left[i] = len(p)
        for j in p: succ[j].append(i)
    pr = [0.0] * n
    for i in range(n - 1, -1, -1): pr[i] = max([pr[s] for s in succ[i]] or [0.0]) + WAKE + us[i] + lat[i]
    pr = [pr[i] + offs.get(ops[i]["name"], 0.0) for i in range(n)]
    rt = [0.0] * n
    fin = [0.0] * n
    free = {}
    ready = {}
    for i in range(n):
        if not left[i]: ready.setdefault(asg[i], []).append(i)
    order = []
    while len(order) < n:
        bt, bq = None, None
        for q in (None, "vector", "scalar", "tensor", "pool", "sync"):
            if ready.get(q):
                t = max(min(rt[i] for i in ready[q]), free.get(q, 0.0))
                if bt is None or t < bt: bt, bq = t, q
        i = min((-pr[i], i) for i in ready[bq] if rt[i] <= bt + 1e-9)[1]
        ready[bq].remove(i)
        f = bt + us[i]
        if bq is not None:
            free[bq] = f
            f += lat[i]
        fin[i] = f
        order.append(i)
        for j in succ[i]:
            rt[j] = max(rt[j], f + WAKE)
            left[j] -= 1
            if not left[j]: ready.setdefault(asg[j], []).append(j)
    return order, max(fin), fin


def rank_program(g, core, T, topo):
    rank = T.rank_of(core)
    if rank is None:
        return
    ops = build(T, rank, topo, core)
    if "p" not in PLAN:
        asg = assign_of(ops, ASG)
        order = plan(ops, asg, OFFS)[0]
        PLAN["p"] = (order, asg, {j: k for k, j in enumerate(order)})
    order, asg, pos = PLAN["p"]
    eng = {"vector": g.vector, "scalar": g.scalar, "tensor": g.tensor, "pool": g, "sync": g.sync}
    count = {}
    done = {}
    clock = {}
    know = {q: {} for q in eng}
    for i in order:
        o, q = ops[i], asg[i]
        if q is None:
            done[i] = o["sem"]; clock[i] = {}
            continue
        need = {}
        for j, kind in o["deps"].items():
            if asg[j] == q and kind != "w" and not ops[j]["sem"] and not o["sem"]: continue
            s, v = done[j]
            if need.get(s, (0, 0))[0] < v: need[s] = (v, j)
        kn = know[q]
        for s, (v, j) in sorted(need.items(), key=lambda z: -pos[z[1][1]]):
            if kn.get(s, 0) >= v: continue
            eng[q].wait_ge(T.sem[s], v)
            for s2, v2 in clock[j].items():
                if kn.get(s2, 0) < v2: kn[s2] = v2
            kn[s] = max(kn.get(s, 0), v)
        ins = [x[2] for x in o["opts"] if x[0] == q][0](eng[q])
        clock[i] = dict(kn)
        if o["sem"]:
            done[i] = o["sem"]
            if o["sem"][0][0] == "d": ins.then_inc(T.sem[o["sem"][0]], o["sem"][1])
        else:
            s = "q_" + q
            count[s] = count.get(s, 0) + 1
            ins.then_inc(T.sem[s], 1)
            done[i] = (s, count[s])
    fin = dict(count)
    for o in ops:
        if o["sem"]: fin[o["sem"][0]] = o["sem"][1]
    for s in sorted(fin): g.wait_ge(T.sem[s], fin[s])
